import numpy as np
import ml_dtypes

BF16 = ml_dtypes.bfloat16


def bf(x):
    return np.asarray(x, np.float32).astype(BF16)


def f32(x):
    return np.asarray(x, np.float32)


def f64(x):
    return np.asarray(x).astype(np.float64)


def striped(idx):
    return np.tile(idx.reshape(-1, 16).T, (8, 1))


def rows(idx, k):
    return np.tile(idx, (k, 1))


def look(tab, idx):
    return np.take_along_axis(f64(tab), rows(idx, len(tab)), axis=1)


K, S, V, N, M = 128, 256, 256, 256, 128


def setup_inputs():
    return {"tab": f32(np.random.standard_normal((K, S))), "qry": f32(np.random.standard_normal((K, V))), "w": bf(np.random.uniform(0.0, 1.0, (K, M)) / K), "offs": striped(np.random.randint(0, S, N))}


def reference(tab, qry, w, offs):
    idx = offs[:16].T.reshape(-1)
    x = (look(tab, idx) - f64(qry)) ** 2
    y = f64(w).T @ x
    return np.exp(-y)

@@ -1,0 +1,40 @@
+import concourse.mybir as mybir
+
+F32, BF16, U16 = mybir.dt.float32, mybir.dt.bfloat16, mybir.dt.uint16
+SUBTRACT = mybir.AluOpType.subtract
+SQUARE = mybir.ActivationFunctionType.Square
+EXP = mybir.ActivationFunctionType.Exp
+
+ROWS, COLUMNS, LIST, METRICS = 128, 256, 256, 128
+PIECE = LIST // 2
+FLOPS = 2 * ROWS * METRICS * LIST + 2 * ROWS * LIST
+
+
+def tile_lookup_dist_sub_rbf_kernel(tc, tab, qry, w, offs, out):
+    nc = tc.nc
+    with (
+        tc.tile_pool(name="held", bufs=1) as held,
+        tc.tile_pool(name="work", bufs=LIST // PIECE) as work,
+        tc.psum_pool(name="sums", bufs=LIST // PIECE) as sums,
+    ):
+        offsets = held.tile([ROWS, LIST // 16], U16)
+        table = held.tile([ROWS, COLUMNS], F32)
+        queries = held.tile([ROWS, LIST], F32)
+        weights = held.tile([ROWS, METRICS], BF16)
+        nc.sync.dma_start(offsets[:], offs)
+        nc.scalar.dma_start(table[:], tab)
+        nc.sync.dma_start(queries[:], qry)
+        nc.sync.dma_start(weights[:], w)
+
+        for start in range(0, LIST, PIECE):
+            piece = slice(start, start + PIECE)
+            entries = offsets[:, start // 16 : (start + PIECE) // 16]
+            difference = work.tile([ROWS, PIECE], F32)
+            nc.vector.tensor_tensor(difference[:], table[:].indirect(entries), queries[:, piece], SUBTRACT)
+            squared = work.tile([ROWS, PIECE], BF16)
+            nc.scalar.activation(squared[:], difference[:], SQUARE)
+            distance = sums.tile([METRICS, PIECE], F32)
+            nc.tensor.matmul(distance[:], weights[:], squared[:], start=True, stop=True)
+            kernel_value = work.tile([METRICS, PIECE], F32)
+            nc.scalar.activation(kernel_value[:], distance[:], EXP, scale=-1.0)
+            nc.sync.dma_start(out[:, piece], kernel_value[:])

@@ -19,18 +19,21 @@ def tile_lookup_dist_sub_rbf_kernel(tc, tab, qry, w, offs, out):
     ):
         offsets = held.tile([ROWS, LIST // 16], U16)
         table = held.tile([ROWS, COLUMNS], F32)
-        queries = held.tile([ROWS, LIST], F32)
         weights = held.tile([ROWS, METRICS], BF16)
+        nc.sync.dma_start(table[:], tab)
         nc.sync.dma_start(offsets[:], offs)
-        nc.scalar.dma_start(table[:], tab)
-        nc.sync.dma_start(queries[:], qry)
+        pieces = [slice(start, start + PIECE) for start in range(0, LIST, PIECE)]
+        queries = []
+        for piece in pieces:
+            loaded = held.tile([ROWS, PIECE], F32, name=f"queries_{piece.start}")
+            nc.scalar.dma_start(loaded[:], qry[:, piece])
+            queries.append(loaded)
         nc.sync.dma_start(weights[:], w)
 
-        for start in range(0, LIST, PIECE):
-            piece = slice(start, start + PIECE)
-            entries = offsets[:, start // 16 : (start + PIECE) // 16]
+        for piece, query in zip(pieces, queries):
+            entries = offsets[:, piece.start // 16 : piece.stop // 16]
             difference = work.tile([ROWS, PIECE], F32)
-            nc.vector.tensor_tensor(difference[:], table[:].indirect(entries), queries[:, piece], SUBTRACT)
+            nc.vector.tensor_tensor(difference[:], table[:].indirect(entries), query[:], SUBTRACT)
             squared = work.tile([ROWS, PIECE], BF16)
             nc.scalar.activation(squared[:], difference[:], SQUARE)
             distance = sums.tile([METRICS, PIECE], F32)

import concourse.mybir as mybir

F32, BF16, U16 = mybir.dt.float32, mybir.dt.bfloat16, mybir.dt.uint16
SUBTRACT = mybir.AluOpType.subtract
SQUARE = mybir.ActivationFunctionType.Square
EXP = mybir.ActivationFunctionType.Exp

ROWS, COLUMNS, LIST, METRICS = 128, 256, 256, 128
PIECE = LIST // 2
FLOPS = 2 * ROWS * METRICS * LIST + 2 * ROWS * LIST


def tile_lookup_dist_sub_rbf_kernel(tc, tab, qry, w, offs, out):
    nc = tc.nc
    with (
        tc.tile_pool(name="held", bufs=1) as held,
        tc.tile_pool(name="work", bufs=LIST // PIECE) as work,
        tc.psum_pool(name="sums", bufs=LIST // PIECE) as sums,
    ):
        offsets = held.tile([ROWS, LIST // 16], U16)
        table = held.tile([ROWS, COLUMNS], F32)
        weights = held.tile([ROWS, METRICS], BF16)
        nc.sync.dma_start(table[:], tab)
        nc.sync.dma_start(offsets[:], offs)
        pieces = [slice(start, start + PIECE) for start in range(0, LIST, PIECE)]
        queries = []
        for piece in pieces:
            loaded = held.tile([ROWS, PIECE], F32, name=f"queries_{piece.start}")
            nc.scalar.dma_start(loaded[:], qry[:, piece])
            queries.append(loaded)
        nc.sync.dma_start(weights[:], w)

        for piece, query in zip(pieces, queries):
            entries = offsets[:, piece.start // 16 : piece.stop // 16]
            difference = work.tile([ROWS, PIECE], F32)
            nc.vector.tensor_tensor(difference[:], table[:].indirect(entries), query[:], SUBTRACT)
            squared = work.tile([ROWS, PIECE], BF16)
            nc.scalar.activation(squared[:], difference[:], SQUARE)
            distance = sums.tile([METRICS, PIECE], F32)
            nc.tensor.matmul(distance[:], weights[:], squared[:], start=True, stop=True)
            kernel_value = work.tile([METRICS, PIECE], F32)
            nc.scalar.activation(kernel_value[:], distance[:], EXP, scale=-1.0)
            nc.sync.dma_start(out[:, piece], kernel_value[:])
